import numpy as np
import ml_dtypes


def mxq(x, axis, fmt="e4m3"):
    dtype, down = {"e4m3": (ml_dtypes.float8_e4m3fn, 7), "e5m2": (ml_dtypes.float8_e5m2, 14)}[fmt]
    v = np.moveaxis(np.asarray(x, np.float32).astype(ml_dtypes.bfloat16).astype(np.float64), axis, -1)
    blocks = v.reshape(v.shape[:-1] + (-1, 32))
    amax = np.abs(blocks).max(-1, keepdims=True)
    byte = np.maximum(np.where(amax > 0, np.frexp(amax)[1] - 1 + 127, 0) - down, 1)
    scale = np.exp2(byte - 127.0)
    codes = (blocks / scale).astype(np.float32).astype(dtype).astype(np.float64)
    return np.moveaxis((codes * scale).reshape(v.shape), -1, axis)


WIDE = False


def mx_kscale(k):
    if not WIDE:
        return np.ones(k)
    levels = np.array([10, -10, 5, -5, 0])
    if k % 512:
        return np.exp2(np.random.permutation(np.resize(levels, k // 32))).repeat(32)
    a = np.empty((k // 512, 16))
    for p in range(k // 512):
        a[p, :8] = np.random.permutation(np.resize(levels, 8))
        for g in range(8):
            far = levels[np.abs(levels - a[p, g]) >= 10]
            a[p, g + 8] = far[np.random.randint(len(far))]
    return np.exp2(a.ravel()).repeat(32)


def f64(x):
    return np.asarray(x).astype(np.float64)


def striped(idx):
    return np.tile(np.asarray(idx).reshape(-1, 16).T, (8, 1)).astype(np.uint16)


def unstriped(offs):
    return offs[:16].T.reshape(-1).astype(np.int64)


E2M1 = np.array([0.0, 0.5, 1.0, 1.5, 2.0, 3.0, 4.0, 6.0, -0.0, -0.5, -1.0, -1.5, -2.0, -3.0, -4.0, -6.0])


def pack_weight(w, fmt):
    k, n = w.shape
    w = f64(np.asarray(w, np.float32).astype(ml_dtypes.bfloat16)).reshape(k // 32, 32, n)
    amax = np.abs(w).max(1)
    if fmt == "e4m3":
        byte = np.frexp(amax)[1] - 1 + 127 - 7
    else:
        mant, ex = np.frexp(amax / 6.0)
        byte = np.where(mant > 0.5, ex, ex - 1) + 127
    byte = np.clip(np.where(amax > 0, byte, 1), 1, 254)
    scaled = (w * np.exp2(127.0 - byte)[:, None, :]).reshape(k, n).astype(np.float32)
    by_word = np.ascontiguousarray(scaled.reshape(k // 512, 128, 4, n).transpose(0, 1, 3, 2))
    if fmt == "e4m3":
        words = by_word.astype(ml_dtypes.float8_e4m3fn).view(np.uint8)
    else:
        c = by_word.astype(ml_dtypes.float4_e2m1fn).view(np.uint8) & 0xF
        words = (c[..., 0::2] | (c[..., 1::2] << 4)).reshape(k // 512, 128, 2 * n)
    return np.ascontiguousarray(words), np.ascontiguousarray(byte.astype(np.uint8).reshape(k // 512, 16, n))


def unpack_weight(words, scales, fmt):
    g, _, n = scales.shape
    words = np.ascontiguousarray(words).reshape(g, 128, n, -1)
    if fmt == "e4m3":
        vals = words.view(ml_dtypes.float8_e4m3fn).astype(np.float64)
    else:
        nib = np.empty((g, 128, n, 4), np.uint8)
        nib[..., 0::2] = words & 0xF
        nib[..., 1::2] = words >> 4
        vals = E2M1[nib]
    vals = vals * np.repeat(np.exp2(scales.astype(np.float64) - 127.0), 8, axis=1)[..., None]
    return vals.transpose(0, 1, 3, 2).reshape(g * 512, n)


def bf(x):
    return np.asarray(x, np.float32).astype(ml_dtypes.bfloat16)


def planes(Y):
    r, m = Y.shape
    b = f64(bf(Y)).reshape(r // 32, 32, m)
    amax = np.abs(b).max(1)
    byte = np.clip(np.where(amax > 0, np.frexp(amax)[1] - 1 + 127 - 7, 1), 1, 254)
    codes = (b * np.exp2(127.0 - byte)[:, None, :]).reshape(r, m).astype(np.float32).astype(ml_dtypes.float8_e4m3fn).view(np.uint8)
    words = codes.reshape(r // 512, 128, 4, m).transpose(0, 1, 3, 2)
    return np.ascontiguousarray(words), np.ascontiguousarray(byte.astype(np.uint8).reshape(r // 512, 16, m))


D, T, I, Q, E, Z, M, C = 512, 2048, 512, 256, 512, 1024, 1024, 512


def setup_inputs():
    n = np.random.standard_normal
    idx = np.random.permutation(T)[:I]
    idx2 = np.random.permutation(Z)[:I]
    idx3 = np.random.permutation(Z)[:I]
    idx4 = np.random.permutation(M)[:Q]
    fd = mx_kscale(D)
    fi = mx_kscale(I)
    fc = mx_kscale(C)
    ti = np.ones(T)
    ti[idx] = fi
    keysp = pack_weight(n((D, T)) / fd[:, None], "e2m1")
    return {
        "query": (n((D, Q)) * 1.0 / np.sqrt(D) * fd[:, None]).astype(np.float32),
        "keys_words": keysp[0],
        "keys_scales": keysp[1],
        "os": (np.random.uniform(0.02, 0.08, (1, I)) * fi).astype(np.float32),
        "vals": (n((E, T)) / ti).astype(np.float32),
        "wm": (n((C, E)) * 1.0 / np.sqrt(C) * fc[:, None]).astype(np.float32),
        "mstore": (n((C, M)) / fc[:, None]).astype(np.float32),
        "offs": striped(idx),
        "offs2": striped(idx2),
        "offs3": striped(idx3),
        "offs4": striped(idx4),
    }


def reference(query, keys_words, keys_scales, os, vals, wm, mstore, offs, offs2, offs3, offs4):
    idx = unstriped(offs)
    idx2 = unstriped(offs2)
    idx3 = unstriped(offs3)
    idx4 = unstriped(offs4)
    keysu = unpack_weight(keys_words, keys_scales, "e2m1")
    queryq = mxq(f64(query), 0, "e4m3")
    keysidxg = keysu[:, idx]
    a = queryq.T @ keysidxg
    f0 = np.zeros((Q, Z))
    f0[:, idx2] = a
    s = a + f0[:, idx3]
    w = np.maximum(s, 0.0)
    wo1 = w * f64(os)
    wt1 = wo1.T
    vt1 = f64(vals)[:, idx].T
    vt1q = mxq(vt1, 0, "e4m3")
    wt1q = mxq(wt1, 0, "e4m3")
    o = vt1q.T @ wt1q
    wmq = mxq(f64(wm), 0, "e4m3")
    mstoreq = mxq(f64(mstore), 0, "e4m3")
    me = wmq.T @ mstoreq
    y = np.maximum(o, me[:, idx4])
    words, scales = planes(y)
    return y, words, scales

@@ -1,0 +1,235 @@
+from contextlib import ExitStack
+
+import concourse.mybir as mybir
+from concourse.masks import make_identity
+
+D, T, I, Q, E, Z, M, C = 512, 2048, 512, 256, 512, 1024, 1024, 512
+FLOPS = 2 * (D * Q * I + I * E * Q + C * E * M)
+
+F32 = mybir.dt.float32
+BF16 = mybir.dt.bfloat16
+I32 = mybir.dt.int32
+U32 = mybir.dt.uint32
+U16 = mybir.dt.uint16
+U8 = mybir.dt.uint8
+E4M3 = mybir.dt.float8_e4m3fn_x4
+E2M1 = mybir.dt.float4_e2m1fn_x4
+COPY = mybir.ActivationFunctionType.Copy
+MAX = mybir.AluOpType.max
+MULT = mybir.AluOpType.mult
+
+P = 128
+PACK = 4
+BANK = 512
+LANES = 16
+
+
+def tile_attend_passedthrough_memorylarger_lean_pl_kernel(
+    tc, query, keys_words, keys_scales, slot_factor, vals, wm, mstore, offs, offs2, offs3, offs4, out_0, out_1, out_2
+):
+    nc = tc.nc
+
+    with ExitStack() as ctx:
+        sb = ctx.enter_context(tc.tile_pool(name="sb", bufs=1))
+        ps = ctx.enter_context(tc.psum_pool(name="ps", bufs=1))
+
+        def new_tile(shape, dtype, name, tag=""):
+            return sb.tile(shape, dtype, name=name, tag=tag or name, align_bytes=64)
+
+        def bank(shape, number, name):
+            return ps.tile(shape, F32, name=name, tag="bank%d" % number)
+
+        def interleave(engine_copy, dst, src):
+            engine_copy(
+                out=dst.rearrange("p (c i) j -> p c j i", i=PACK),
+                in_=src.rearrange("p j (c i) -> p c j i", i=PACK),
+            )
+
+        def quantise(src, columns, name):
+            codes = new_tile([P, columns], U32, name + "_codes")
+            scales = new_tile([P, columns], U8, name + "_scales")
+            nc.vector.quantize_mx(out=codes[:].bitcast(E4M3), scales=scales[:], in_=src)
+            return codes, scales
+
+        def product(out, left, cols, right):
+            nc.tensor.matmul_mx(
+                out=out, lhsT=left[0][:, cols].bitcast(E4M3), lhsT_scale=left[1][:, cols],
+                rhs=right[0], rhs_scale=right[1], start=True, stop=True,
+            )
+
+        def gather(on_vector, dst, window, offsets):
+            if on_vector:
+                nc.vector.tensor_copy(dst, window.indirect(offsets))
+            else:
+                nc.scalar.activation(dst, window.indirect(offsets), COPY)
+
+        def evacuate(on_vector, dst, src):
+            if on_vector:
+                nc.vector.tensor_copy(out=dst, in_=src)
+            else:
+                nc.scalar.copy(out=dst, in_=src)
+
+        key_bytes = new_tile([P, T], U8, "key_bytes")
+        nc.vector.memset(key_bytes[:].bitcast(I32), 0)
+        key_words = new_tile([P, T], U16, "key_words")
+        nc.sync.dma_start(key_words[:].bitcast(I32), keys_words[0].bitcast(I32))
+        idx = new_tile([P, I // LANES], U16, "idx")
+        nc.sync.dma_start(idx[:], offs)
+        for r in range(4):
+            nc.sync.dma_start(key_bytes[r:P:32, :].bitcast(I32), keys_scales[0, r:16:4, :].bitcast(I32))
+        q_raw = new_tile([P, PACK, Q], F32, "q_raw")
+        nc.sync.dma_start(q_raw[:], query.rearrange("(p j) q -> p j q", j=PACK))
+        wm_raw = new_tile([P, PACK, E], F32, "wm_raw")
+        nc.sync.dma_start(wm_raw[:], wm.rearrange("(p j) e -> p j e", j=PACK))
+        idx2 = new_tile([P, I // LANES], U16, "idx2")
+        nc.sync.dma_start(idx2[:], offs2)
+        idx3 = new_tile([P, I // LANES], U16, "idx3")
+        nc.sync.dma_start(idx3[:], offs3)
+        ms_rows = mstore.rearrange("(p j) m -> p j m", j=PACK)
+        ms_raw = []
+        for h in range(2):
+            ms_raw.append(new_tile([P, PACK, BANK], F32, "ms_raw%d" % h))
+            nc.sync.dma_start(ms_raw[h][:], ms_rows[:, :, h * BANK : (h + 1) * BANK])
+        factor = new_tile([P, PACK], F32, "factor")
+        nc.sync.dma_start(factor[:], slot_factor.rearrange("o (p t) -> p (o t)", t=PACK))
+        idx4 = new_tile([P, Q // LANES], U16, "idx4")
+        nc.sync.dma_start(idx4[:], offs4)
+        val_rows = vals.rearrange("(p j) t -> p j t", j=PACK)
+        val_pool = []
+        for j in range(PACK):
+            val_pool.append(new_tile([P, T], F32, "val_pool%d" % j))
+            nc.sync.dma_start(val_pool[j][:], val_rows[:, j, :])
+
+        ident = new_tile([P, P], F32, "ident")
+        make_identity(nc, ident[:])
+        places = []
+        for qt in range(2):
+            places.append(new_tile([P, Z], F32, "places%d" % qt))
+            nc.gpsimd.memset(places[qt][:], 0.0)
+
+        got_words = new_tile([P, I], U16, "got_words")
+        nc.vector.tensor_copy(got_words[:], key_words[:].indirect(idx[:]))
+        got_bytes = new_tile([P, I], U8, "got_bytes")
+        nc.vector.tensor_copy(got_bytes[:], key_bytes[:].indirect(idx[:]))
+        a_sb = []
+        for qt in range(2):
+            q_bf = new_tile([P, P, PACK], BF16, "q_bf%d" % qt)
+            interleave(nc.scalar.copy, q_bf[:], q_raw[:, :, qt * P : (qt + 1) * P])
+            q_mx = quantise(q_bf[:].rearrange("p q j -> p (q j)"), P, "q%d" % qt)
+            a_ps = bank([P, BANK], qt, "a_ps%d" % qt)
+            product(a_ps[:], q_mx, slice(0, P), (got_words[:].bitcast(E2M1), got_bytes[:]))
+            a_sb.append(new_tile([P, I], F32, "a_sb%d" % qt))
+            nc.vector.tensor_copy(out=a_sb[qt][:], in_=a_ps[:])
+
+        wm_bf = new_tile([P, PACK, P, PACK], BF16, "wm_bf")
+        nc.scalar.copy(
+            out=wm_bf[:].rearrange("p t m j -> p m j t"),
+            in_=wm_raw[:].rearrange("p j (m t) -> p m j t", t=PACK),
+        )
+
+        nc.vector.tensor_copy(places[0][:].indirect(idx2[:]), a_sb[0][:])
+        half = I // 2
+        for s in range(2):
+            nc.scalar.activation(
+                places[1][:].indirect(idx2[:, s * half // LANES : (s + 1) * half // LANES]),
+                a_sb[1][:, s * half : (s + 1) * half], COPY,
+            )
+
+        s_ps = []
+        for qt in range(2):
+            s_ps.append(bank([P, PACK, P], qt, "s_ps%d" % qt))
+            for t in range(PACK):
+                nc.tensor.matmul(s_ps[qt][:, t, :], lhsT=a_sb[qt][:, t::PACK], rhs=ident[:], is_transpose=True, start=(t == 0), stop=False)
+
+        wm_mx = quantise(wm_bf[:].rearrange("p t m j -> p (t m j)"), E, "wm")
+        ms_bf = [new_tile([P, BANK, PACK], BF16, "ms_bf%d" % h) for h in range(2)]
+        interleave(nc.vector.tensor_copy, ms_bf[0][:], ms_raw[0][:])
+
+        def look_up_places(qt):
+            passed = new_tile([P, I], F32, "passed%d" % qt, tag="a_sb1" if qt == 0 else "")
+            gather(qt == 1, passed[:], places[qt][:], idx3[:])
+            for t in range(PACK):
+                nc.tensor.matmul(s_ps[qt][:, t, :], lhsT=passed[:, t::PACK], rhs=ident[:], is_transpose=True, start=False, stop=(t == PACK - 1))
+
+        w_bf = new_tile([P, Q, PACK], BF16, "w_bf")
+
+        def weigh(qt):
+            nc.vector.scalar_tensor_tensor(
+                out=w_bf[:, qt * P : (qt + 1) * P, :], in0=s_ps[qt][:].rearrange("p t q -> p q t"), scalar=0.0,
+                in1=factor[:].unsqueeze(1).to_broadcast([P, P, PACK]), op0=MAX, op1=MULT,
+            )
+
+        def memory_product(h, j):
+            me_ps = bank([P, BANK], (2 + j) if h == 0 else (6, 7, 2, 3)[j], "me_ps%d_%d" % (h, j))
+            product(me_ps[:], wm_mx, slice(j * P, (j + 1) * P), (ms_mx[h][0][:].bitcast(E4M3), ms_mx[h][1][:]))
+            return me_ps
+
+        look_up_places(0)
+        ms_mx = [quantise(ms_bf[0][:].rearrange("p m j -> p (m j)"), BANK, "ms0")]
+        me_first = [memory_product(0, j) for j in range(PACK)]
+        look_up_places(1)
+        interleave(nc.vector.tensor_copy, ms_bf[1][:], ms_raw[1][:])
+        weigh(0)
+        ms_mx.append(quantise(ms_bf[1][:].rearrange("p m j -> p (m j)"), BANK, "ms1"))
+        weigh(1)
+
+        got_vals = [new_tile([P, I], BF16, "got_vals%d" % j) for j in range(PACK)]
+        for j in range(2):
+            gather(False, got_vals[j][:], val_pool[j][:], idx[:])
+        mem = new_tile([P, PACK * M], F32, "mem", tag="val_pool1")
+        for j in range(PACK):
+            evacuate(False, mem[:, j * M : j * M + BANK], me_first[j][:])
+
+        def turn(j):
+            pairs = got_vals[j][:].bitcast(F32)
+            vt_ps = bank([P, 2, P], (0, 1, 4, 5)[j], "vt_ps%d" % j)
+            for u in range(2):
+                nc.tensor.transpose(vt_ps[:, u, :], pairs[:, u::2], ident[:])
+            vt_words = new_tile([P, P, 2], F32, "vt_words%d" % j)
+            evacuate(j < 2, vt_words[:], vt_ps[:].rearrange("p u m -> p m u"))
+            return vt_words
+
+        def quantise_values(j, vt_words):
+            return quantise(vt_words[:].rearrange("p m u -> p (m u)").bitcast(BF16), P, "vt%d" % j)
+
+        words0 = turn(0)
+        w_mx = quantise(w_bf[:].rearrange("p q t -> p (q t)"), Q, "w")
+        words1 = turn(1)
+        vt_mx = [quantise_values(0, words0), quantise_values(1, words1)]
+
+        me_second = [memory_product(1, j) for j in range(PACK)]
+        for j in range(2):
+            evacuate(True, mem[:, j * M + BANK : (j + 1) * M], me_second[j][:])
+        gather(False, got_vals[2][:], val_pool[2][:], idx[:])
+        gather(False, got_vals[3][:], val_pool[3][:], idx[:])
+        for j in range(2, PACK):
+            evacuate(True, mem[:, j * M + BANK : (j + 1) * M], me_second[j][:])
+        for j in range(2, PACK):
+            vt_mx.append(quantise_values(j, turn(j)))
+
+        late = new_tile([P, 3, Q], F32, "late", tag="val_pool3")
+        clk0 = new_tile([P, 1], BF16, "clk0")
+        nc.gpsimd.tensor_copy(out=clk0[:], in_=got_vals[3][:, 0:1])
+        clk1 = new_tile([P, 1], U32, "clk1")
+        nc.gpsimd.tensor_copy(out=clk1[:], in_=vt_mx[3][0][:, 0:1])
+        y = new_tile([P, PACK, Q], F32, "y")
+        out_rows = out_0.rearrange("(p j) q -> p j q", j=PACK)
+        for j in range(PACK):
+            recalled = new_tile([P, Q], F32, "recalled%d" % j) if j < 1 else late[:, j - 1, :]
+            gather(j < 1, recalled[:], mem[:, j * M : (j + 1) * M], idx4[:])
+            o_ps = bank([P, Q], (4, 5, 6, 7)[j], "o_ps%d" % j)
+            product(o_ps[:], vt_mx[j], slice(0, P), (w_mx[0][:].bitcast(E4M3), w_mx[1][:]))
+            nc.vector.tensor_tensor(out=y[:, j, :], in0=o_ps[:], in1=recalled[:], op=MAX)
+            if j % 2 == 1:
+                nc.sync.dma_start(out_rows[:, j - 1 : j + 1, :], y[:, j - 1 : j + 1, :])
+
+        y_bf = new_tile([P, Q, PACK], BF16, "y_bf")
+        interleave(nc.vector.tensor_copy, y_bf[:], y[:])
+        y_codes, y_scales = quantise(y_bf[:].rearrange("p q j -> p (q j)"), Q, "y")
+        nc.sync.dma_start(out_1[0].rearrange("p c r -> p (c r)").bitcast(I32), y_codes[:].bitcast(I32))
+        for quad in range(4):
+            queue = nc.scalar if quad % 2 == 0 else nc.sync
+            queue.dma_start(
+                out_2[0, 4 * quad : 4 * quad + 4, :].bitcast(I32),
+                y_scales[32 * quad : 32 * quad + 4, :].bitcast(I32),
+            )

@@ -22,6 +22,7 @@ P = 128
 PACK = 4
 BANK = 512
 LANES = 16
+Y_SCALAR = 96
 
 
 def tile_attend_passedthrough_memorylarger_lean_pl_kernel(
@@ -123,8 +124,8 @@ def tile_attend_passedthrough_memorylarger_lean_pl_kernel(
 
         wm_bf = new_tile([P, PACK, P, PACK], BF16, "wm_bf")
         nc.scalar.copy(
-            out=wm_bf[:].rearrange("p t m j -> p m j t"),
-            in_=wm_raw[:].rearrange("p j (m t) -> p m j t", t=PACK),
+            out=wm_bf[:].rearrange("p (a b) m j -> p a m j b", b=2),
+            in_=wm_raw[:].rearrange("p j (m a b) -> p a m j b", a=2, b=2),
         )
 
         nc.vector.tensor_copy(places[0][:].indirect(idx2[:]), a_sb[0][:])
@@ -208,23 +209,27 @@ def tile_attend_passedthrough_memorylarger_lean_pl_kernel(
             vt_mx.append(quantise_values(j, turn(j)))
 
         late = new_tile([P, 3, Q], F32, "late", tag="val_pool3")
-        clk0 = new_tile([P, 1], BF16, "clk0")
-        nc.gpsimd.tensor_copy(out=clk0[:], in_=got_vals[3][:, 0:1])
-        clk1 = new_tile([P, 1], U32, "clk1")
-        nc.gpsimd.tensor_copy(out=clk1[:], in_=vt_mx[3][0][:, 0:1])
         y = new_tile([P, PACK, Q], F32, "y")
         out_rows = out_0.rearrange("(p j) q -> p j q", j=PACK)
+        w_operand = (w_mx[0][:].bitcast(E4M3), w_mx[1][:])
+        o_first = bank([P, 2, Q], 4, "o_first")
+        for j in range(2):
+            product(o_first[:, j, :], vt_mx[j], slice(0, P), w_operand)
         for j in range(PACK):
             recalled = new_tile([P, Q], F32, "recalled%d" % j) if j < 1 else late[:, j - 1, :]
             gather(j < 1, recalled[:], mem[:, j * M : (j + 1) * M], idx4[:])
-            o_ps = bank([P, Q], (4, 5, 6, 7)[j], "o_ps%d" % j)
-            product(o_ps[:], vt_mx[j], slice(0, P), (w_mx[0][:].bitcast(E4M3), w_mx[1][:]))
-            nc.vector.tensor_tensor(out=y[:, j, :], in0=o_ps[:], in1=recalled[:], op=MAX)
+            if j < 2:
+                o_ps = o_first[:, j, :]
+            else:
+                o_ps = bank([P, Q], 4 + j, "o_ps%d" % j)[:]
+                product(o_ps, vt_mx[j], slice(0, P), w_operand)
+            nc.vector.tensor_tensor(out=y[:, j, :], in0=o_ps, in1=recalled[:], op=MAX)
             if j % 2 == 1:
                 nc.sync.dma_start(out_rows[:, j - 1 : j + 1, :], y[:, j - 1 : j + 1, :])
 
         y_bf = new_tile([P, Q, PACK], BF16, "y_bf")
-        interleave(nc.vector.tensor_copy, y_bf[:], y[:])
+        interleave(nc.scalar.copy, y_bf[:, :Y_SCALAR, :], y[:, :, :Y_SCALAR])
+        interleave(nc.vector.tensor_copy, y_bf[:, Y_SCALAR:, :], y[:, :, Y_SCALAR:])
         y_codes, y_scales = quantise(y_bf[:].rearrange("p q j -> p (q j)"), Q, "y")
         nc.sync.dma_start(out_1[0].rearrange("p c r -> p (c r)").bitcast(I32), y_codes[:].bitcast(I32))
         for quad in range(4):

@@ -20,6 +20,8 @@ MULT = mybir.AluOpType.mult
 
 P = 128
 PACK = 4
+QUAD = 32
+BLOCK = 32
 BANK = 512
 LANES = 16
 Y_SCALAR = 96
@@ -34,8 +36,8 @@ def tile_attend_passedthrough_memorylarger_lean_pl_kernel(
         sb = ctx.enter_context(tc.tile_pool(name="sb", bufs=1))
         ps = ctx.enter_context(tc.psum_pool(name="ps", bufs=1))
 
-        def new_tile(shape, dtype, name, tag=""):
-            return sb.tile(shape, dtype, name=name, tag=tag or name, align_bytes=64)
+        def new_tile(shape, dtype, name, reuse=""):
+            return sb.tile(shape, dtype, name=name, tag=reuse or name, align_bytes=64)
 
         def bank(shape, number, name):
             return ps.tile(shape, F32, name=name, tag="bank%d" % number)
@@ -52,10 +54,13 @@ def tile_attend_passedthrough_memorylarger_lean_pl_kernel(
             nc.vector.quantize_mx(out=codes[:].bitcast(E4M3), scales=scales[:], in_=src)
             return codes, scales
 
-        def product(out, left, cols, right):
+        def moving(quantised):
+            return quantised[0][:].bitcast(E4M3), quantised[1][:]
+
+        def product(out, stationary, cols, moving_operand):
             nc.tensor.matmul_mx(
-                out=out, lhsT=left[0][:, cols].bitcast(E4M3), lhsT_scale=left[1][:, cols],
-                rhs=right[0], rhs_scale=right[1], start=True, stop=True,
+                out=out, lhsT=stationary[0][:, cols].bitcast(E4M3), lhsT_scale=stationary[1][:, cols],
+                rhs=moving_operand[0], rhs_scale=moving_operand[1], start=True, stop=True,
             )
 
         def gather(on_vector, dst, window, offsets):
@@ -76,8 +81,8 @@ def tile_attend_passedthrough_memorylarger_lean_pl_kernel(
         nc.sync.dma_start(key_words[:].bitcast(I32), keys_words[0].bitcast(I32))
         idx = new_tile([P, I // LANES], U16, "idx")
         nc.sync.dma_start(idx[:], offs)
-        for r in range(4):
-            nc.sync.dma_start(key_bytes[r:P:32, :].bitcast(I32), keys_scales[0, r:16:4, :].bitcast(I32))
+        for r in range(PACK):
+            nc.sync.dma_start(key_bytes[r:P:QUAD, :].bitcast(I32), keys_scales[0, r : D // BLOCK : PACK, :].bitcast(I32))
         q_raw = new_tile([P, PACK, Q], F32, "q_raw")
         nc.sync.dma_start(q_raw[:], query.rearrange("(p j) q -> p j q", j=PACK))
         wm_raw = new_tile([P, PACK, E], F32, "wm_raw")
@@ -140,17 +145,22 @@ def tile_attend_passedthrough_memorylarger_lean_pl_kernel(
         for qt in range(2):
             s_ps.append(bank([P, PACK, P], qt, "s_ps%d" % qt))
             for t in range(PACK):
-                nc.tensor.matmul(s_ps[qt][:, t, :], lhsT=a_sb[qt][:, t::PACK], rhs=ident[:], is_transpose=True, start=(t == 0), stop=False)
+                nc.tensor.matmul(
+                    s_ps[qt][:, t, :], lhsT=a_sb[qt][:, t::PACK], rhs=ident[:], is_transpose=True, start=(t == 0), stop=False
+                )
 
         wm_mx = quantise(wm_bf[:].rearrange("p t m j -> p (t m j)"), E, "wm")
         ms_bf = [new_tile([P, BANK, PACK], BF16, "ms_bf%d" % h) for h in range(2)]
         interleave(nc.vector.tensor_copy, ms_bf[0][:], ms_raw[0][:])
 
         def look_up_places(qt):
-            passed = new_tile([P, I], F32, "passed%d" % qt, tag="a_sb1" if qt == 0 else "")
+            passed = new_tile([P, I], F32, "passed%d" % qt, reuse="a_sb1" if qt == 0 else "")
             gather(qt == 1, passed[:], places[qt][:], idx3[:])
             for t in range(PACK):
-                nc.tensor.matmul(s_ps[qt][:, t, :], lhsT=passed[:, t::PACK], rhs=ident[:], is_transpose=True, start=False, stop=(t == PACK - 1))
+                nc.tensor.matmul(
+                    s_ps[qt][:, t, :], lhsT=passed[:, t::PACK], rhs=ident[:], is_transpose=True, start=False,
+                    stop=(t == PACK - 1),
+                )
 
         w_bf = new_tile([P, Q, PACK], BF16, "w_bf")
 
@@ -161,8 +171,8 @@ def tile_attend_passedthrough_memorylarger_lean_pl_kernel(
             )
 
         def memory_product(h, j):
-            me_ps = bank([P, BANK], (2 + j) if h == 0 else (6, 7, 2, 3)[j], "me_ps%d_%d" % (h, j))
-            product(me_ps[:], wm_mx, slice(j * P, (j + 1) * P), (ms_mx[h][0][:].bitcast(E4M3), ms_mx[h][1][:]))
+            me_ps = bank([P, BANK], 2 + (PACK * h + j) % 6, "me_ps%d_%d" % (h, j))
+            product(me_ps[:], wm_mx, slice(j * P, (j + 1) * P), moving(ms_mx[h]))
             return me_ps
 
         look_up_places(0)
@@ -175,27 +185,26 @@ def tile_attend_passedthrough_memorylarger_lean_pl_kernel(
         weigh(1)
 
         got_vals = [new_tile([P, I], BF16, "got_vals%d" % j) for j in range(PACK)]
-        for j in range(2):
-            gather(False, got_vals[j][:], val_pool[j][:], idx[:])
-        mem = new_tile([P, PACK * M], F32, "mem", tag="val_pool1")
+        gather(False, got_vals[0][:], val_pool[0][:], idx[:])
+        mem = new_tile([P, PACK * M], F32, "mem", reuse="val_pool0")
         for j in range(PACK):
             evacuate(False, mem[:, j * M : j * M + BANK], me_first[j][:])
+        gather(False, got_vals[1][:], val_pool[1][:], idx[:])
 
-        def turn(j):
+        def turn(j, vt_words):
             pairs = got_vals[j][:].bitcast(F32)
-            vt_ps = bank([P, 2, P], (0, 1, 4, 5)[j], "vt_ps%d" % j)
+            vt_ps = bank([P, 2, P], j if j < 2 else j + 2, "vt_ps%d" % j)
             for u in range(2):
                 nc.tensor.transpose(vt_ps[:, u, :], pairs[:, u::2], ident[:])
-            vt_words = new_tile([P, P, 2], F32, "vt_words%d" % j)
-            evacuate(j < 2, vt_words[:], vt_ps[:].rearrange("p u m -> p m u"))
+            evacuate(j < 2, vt_words.rearrange("p (m u) -> p m u", u=2), vt_ps[:].rearrange("p u m -> p m u"))
             return vt_words
 
         def quantise_values(j, vt_words):
-            return quantise(vt_words[:].rearrange("p m u -> p (m u)").bitcast(BF16), P, "vt%d" % j)
+            return quantise(vt_words.bitcast(BF16), P, "vt%d" % j)
 
-        words0 = turn(0)
+        words0 = turn(0, new_tile([P, 2 * P], F32, "vt_words0")[:])
         w_mx = quantise(w_bf[:].rearrange("p q t -> p (q t)"), Q, "w")
-        words1 = turn(1)
+        words1 = turn(1, new_tile([P, 2 * P], F32, "vt_words1")[:])
         vt_mx = [quantise_values(0, words0), quantise_values(1, words1)]
 
         me_second = [memory_product(1, j) for j in range(PACK)]
@@ -205,25 +214,25 @@ def tile_attend_passedthrough_memorylarger_lean_pl_kernel(
         gather(False, got_vals[3][:], val_pool[3][:], idx[:])
         for j in range(2, PACK):
             evacuate(True, mem[:, j * M + BANK : (j + 1) * M], me_second[j][:])
-        for j in range(2, PACK):
-            vt_mx.append(quantise_values(j, turn(j)))
+        late = new_tile([P, PACK, Q], F32, "late", reuse="val_pool3")
+        vt_mx.append(quantise_values(2, turn(2, late[:, 0, :])))
+        vt_mx.append(quantise_values(3, turn(3, new_tile([P, 2 * P], F32, "vt_words3")[:])))
 
-        late = new_tile([P, 3, Q], F32, "late", tag="val_pool3")
         y = new_tile([P, PACK, Q], F32, "y")
         out_rows = out_0.rearrange("(p j) q -> p j q", j=PACK)
-        w_operand = (w_mx[0][:].bitcast(E4M3), w_mx[1][:])
+        w_operand = moving(w_mx)
         o_first = bank([P, 2, Q], 4, "o_first")
         for j in range(2):
             product(o_first[:, j, :], vt_mx[j], slice(0, P), w_operand)
         for j in range(PACK):
-            recalled = new_tile([P, Q], F32, "recalled%d" % j) if j < 1 else late[:, j - 1, :]
-            gather(j < 1, recalled[:], mem[:, j * M : (j + 1) * M], idx4[:])
+            recalled = new_tile([P, Q], F32, "recalled0")[:] if j == 0 else late[:, j, :]
+            gather(j == 0, recalled, mem[:, j * M : (j + 1) * M], idx4[:])
             if j < 2:
                 o_ps = o_first[:, j, :]
             else:
                 o_ps = bank([P, Q], 4 + j, "o_ps%d" % j)[:]
                 product(o_ps, vt_mx[j], slice(0, P), w_operand)
-            nc.vector.tensor_tensor(out=y[:, j, :], in0=o_ps, in1=recalled[:], op=MAX)
+            nc.vector.tensor_tensor(out=y[:, j, :], in0=o_ps, in1=recalled, op=MAX)
             if j % 2 == 1:
                 nc.sync.dma_start(out_rows[:, j - 1 : j + 1, :], y[:, j - 1 : j + 1, :])
 
@@ -232,9 +241,9 @@ def tile_attend_passedthrough_memorylarger_lean_pl_kernel(
         interleave(nc.vector.tensor_copy, y_bf[:, Y_SCALAR:, :], y[:, :, Y_SCALAR:])
         y_codes, y_scales = quantise(y_bf[:].rearrange("p q j -> p (q j)"), Q, "y")
         nc.sync.dma_start(out_1[0].rearrange("p c r -> p (c r)").bitcast(I32), y_codes[:].bitcast(I32))
-        for quad in range(4):
+        for quad in range(P // QUAD):
             queue = nc.scalar if quad % 2 == 0 else nc.sync
             queue.dma_start(
-                out_2[0, 4 * quad : 4 * quad + 4, :].bitcast(I32),
-                y_scales[32 * quad : 32 * quad + 4, :].bitcast(I32),
+                out_2[0, PACK * quad : PACK * (quad + 1), :].bitcast(I32),
+                y_scales[QUAD * quad : QUAD * quad + PACK, :].bitcast(I32),
             )

from contextlib import ExitStack

import concourse.mybir as mybir
from concourse.masks import make_identity

D, T, I, Q, E, Z, M, C = 512, 2048, 512, 256, 512, 1024, 1024, 512
FLOPS = 2 * (D * Q * I + I * E * Q + C * E * M)

F32 = mybir.dt.float32
BF16 = mybir.dt.bfloat16
I32 = mybir.dt.int32
U32 = mybir.dt.uint32
U16 = mybir.dt.uint16
U8 = mybir.dt.uint8
E4M3 = mybir.dt.float8_e4m3fn_x4
E2M1 = mybir.dt.float4_e2m1fn_x4
COPY = mybir.ActivationFunctionType.Copy
MAX = mybir.AluOpType.max
MULT = mybir.AluOpType.mult

P = 128
PACK = 4
QUAD = 32
BLOCK = 32
BANK = 512
LANES = 16
Y_SCALAR = 96


def tile_attend_passedthrough_memorylarger_lean_pl_kernel(
    tc, query, keys_words, keys_scales, slot_factor, vals, wm, mstore, offs, offs2, offs3, offs4, out_0, out_1, out_2
):
    nc = tc.nc

    with ExitStack() as ctx:
        sb = ctx.enter_context(tc.tile_pool(name="sb", bufs=1))
        ps = ctx.enter_context(tc.psum_pool(name="ps", bufs=1))

        def new_tile(shape, dtype, name, reuse=""):
            return sb.tile(shape, dtype, name=name, tag=reuse or name, align_bytes=64)

        def bank(shape, number, name):
            return ps.tile(shape, F32, name=name, tag="bank%d" % number)

        def interleave(engine_copy, dst, src):
            engine_copy(
                out=dst.rearrange("p (c i) j -> p c j i", i=PACK),
                in_=src.rearrange("p j (c i) -> p c j i", i=PACK),
            )

        def quantise(src, columns, name):
            codes = new_tile([P, columns], U32, name + "_codes")
            scales = new_tile([P, columns], U8, name + "_scales")
            nc.vector.quantize_mx(out=codes[:].bitcast(E4M3), scales=scales[:], in_=src)
            return codes, scales

        def moving(quantised):
            return quantised[0][:].bitcast(E4M3), quantised[1][:]

        def product(out, stationary, cols, moving_operand):
            nc.tensor.matmul_mx(
                out=out, lhsT=stationary[0][:, cols].bitcast(E4M3), lhsT_scale=stationary[1][:, cols],
                rhs=moving_operand[0], rhs_scale=moving_operand[1], start=True, stop=True,
            )

        def gather(on_vector, dst, window, offsets):
            if on_vector:
                nc.vector.tensor_copy(dst, window.indirect(offsets))
            else:
                nc.scalar.activation(dst, window.indirect(offsets), COPY)

        def evacuate(on_vector, dst, src):
            if on_vector:
                nc.vector.tensor_copy(out=dst, in_=src)
            else:
                nc.scalar.copy(out=dst, in_=src)

        key_bytes = new_tile([P, T], U8, "key_bytes")
        nc.vector.memset(key_bytes[:].bitcast(I32), 0)
        key_words = new_tile([P, T], U16, "key_words")
        nc.sync.dma_start(key_words[:].bitcast(I32), keys_words[0].bitcast(I32))
        idx = new_tile([P, I // LANES], U16, "idx")
        nc.sync.dma_start(idx[:], offs)
        for r in range(PACK):
            nc.sync.dma_start(key_bytes[r:P:QUAD, :].bitcast(I32), keys_scales[0, r : D // BLOCK : PACK, :].bitcast(I32))
        q_raw = new_tile([P, PACK, Q], F32, "q_raw")
        nc.sync.dma_start(q_raw[:], query.rearrange("(p j) q -> p j q", j=PACK))
        wm_raw = new_tile([P, PACK, E], F32, "wm_raw")
        nc.sync.dma_start(wm_raw[:], wm.rearrange("(p j) e -> p j e", j=PACK))
        idx2 = new_tile([P, I // LANES], U16, "idx2")
        nc.sync.dma_start(idx2[:], offs2)
        idx3 = new_tile([P, I // LANES], U16, "idx3")
        nc.sync.dma_start(idx3[:], offs3)
        ms_rows = mstore.rearrange("(p j) m -> p j m", j=PACK)
        ms_raw = []
        for h in range(2):
            ms_raw.append(new_tile([P, PACK, BANK], F32, "ms_raw%d" % h))
            nc.sync.dma_start(ms_raw[h][:], ms_rows[:, :, h * BANK : (h + 1) * BANK])
        factor = new_tile([P, PACK], F32, "factor")
        nc.sync.dma_start(factor[:], slot_factor.rearrange("o (p t) -> p (o t)", t=PACK))
        idx4 = new_tile([P, Q // LANES], U16, "idx4")
        nc.sync.dma_start(idx4[:], offs4)
        val_rows = vals.rearrange("(p j) t -> p j t", j=PACK)
        val_pool = []
        for j in range(PACK):
            val_pool.append(new_tile([P, T], F32, "val_pool%d" % j))
            nc.sync.dma_start(val_pool[j][:], val_rows[:, j, :])

        ident = new_tile([P, P], F32, "ident")
        make_identity(nc, ident[:])
        places = []
        for qt in range(2):
            places.append(new_tile([P, Z], F32, "places%d" % qt))
            nc.gpsimd.memset(places[qt][:], 0.0)

        got_words = new_tile([P, I], U16, "got_words")
        nc.vector.tensor_copy(got_words[:], key_words[:].indirect(idx[:]))
        got_bytes = new_tile([P, I], U8, "got_bytes")
        nc.vector.tensor_copy(got_bytes[:], key_bytes[:].indirect(idx[:]))
        a_sb = []
        for qt in range(2):
            q_bf = new_tile([P, P, PACK], BF16, "q_bf%d" % qt)
            interleave(nc.scalar.copy, q_bf[:], q_raw[:, :, qt * P : (qt + 1) * P])
            q_mx = quantise(q_bf[:].rearrange("p q j -> p (q j)"), P, "q%d" % qt)
            a_ps = bank([P, BANK], qt, "a_ps%d" % qt)
            product(a_ps[:], q_mx, slice(0, P), (got_words[:].bitcast(E2M1), got_bytes[:]))
            a_sb.append(new_tile([P, I], F32, "a_sb%d" % qt))
            nc.vector.tensor_copy(out=a_sb[qt][:], in_=a_ps[:])

        wm_bf = new_tile([P, PACK, P, PACK], BF16, "wm_bf")
        nc.scalar.copy(
            out=wm_bf[:].rearrange("p (a b) m j -> p a m j b", b=2),
            in_=wm_raw[:].rearrange("p j (m a b) -> p a m j b", a=2, b=2),
        )

        nc.vector.tensor_copy(places[0][:].indirect(idx2[:]), a_sb[0][:])
        half = I // 2
        for s in range(2):
            nc.scalar.activation(
                places[1][:].indirect(idx2[:, s * half // LANES : (s + 1) * half // LANES]),
                a_sb[1][:, s * half : (s + 1) * half], COPY,
            )

        s_ps = []
        for qt in range(2):
            s_ps.append(bank([P, PACK, P], qt, "s_ps%d" % qt))
            for t in range(PACK):
                nc.tensor.matmul(
                    s_ps[qt][:, t, :], lhsT=a_sb[qt][:, t::PACK], rhs=ident[:], is_transpose=True, start=(t == 0), stop=False
                )

        wm_mx = quantise(wm_bf[:].rearrange("p t m j -> p (t m j)"), E, "wm")
        ms_bf = [new_tile([P, BANK, PACK], BF16, "ms_bf%d" % h) for h in range(2)]
        interleave(nc.vector.tensor_copy, ms_bf[0][:], ms_raw[0][:])

        def look_up_places(qt):
            passed = new_tile([P, I], F32, "passed%d" % qt, reuse="a_sb1" if qt == 0 else "")
            gather(qt == 1, passed[:], places[qt][:], idx3[:])
            for t in range(PACK):
                nc.tensor.matmul(
                    s_ps[qt][:, t, :], lhsT=passed[:, t::PACK], rhs=ident[:], is_transpose=True, start=False,
                    stop=(t == PACK - 1),
                )

        w_bf = new_tile([P, Q, PACK], BF16, "w_bf")

        def weigh(qt):
            nc.vector.scalar_tensor_tensor(
                out=w_bf[:, qt * P : (qt + 1) * P, :], in0=s_ps[qt][:].rearrange("p t q -> p q t"), scalar=0.0,
                in1=factor[:].unsqueeze(1).to_broadcast([P, P, PACK]), op0=MAX, op1=MULT,
            )

        def memory_product(h, j):
            me_ps = bank([P, BANK], 2 + (PACK * h + j) % 6, "me_ps%d_%d" % (h, j))
            product(me_ps[:], wm_mx, slice(j * P, (j + 1) * P), moving(ms_mx[h]))
            return me_ps

        look_up_places(0)
        ms_mx = [quantise(ms_bf[0][:].rearrange("p m j -> p (m j)"), BANK, "ms0")]
        me_first = [memory_product(0, j) for j in range(PACK)]
        look_up_places(1)
        interleave(nc.vector.tensor_copy, ms_bf[1][:], ms_raw[1][:])
        weigh(0)
        ms_mx.append(quantise(ms_bf[1][:].rearrange("p m j -> p (m j)"), BANK, "ms1"))
        weigh(1)

        got_vals = [new_tile([P, I], BF16, "got_vals%d" % j) for j in range(PACK)]
        gather(False, got_vals[0][:], val_pool[0][:], idx[:])
        mem = new_tile([P, PACK * M], F32, "mem", reuse="val_pool0")
        for j in range(PACK):
            evacuate(False, mem[:, j * M : j * M + BANK], me_first[j][:])
        gather(False, got_vals[1][:], val_pool[1][:], idx[:])

        def turn(j, vt_words):
            pairs = got_vals[j][:].bitcast(F32)
            vt_ps = bank([P, 2, P], j if j < 2 else j + 2, "vt_ps%d" % j)
            for u in range(2):
                nc.tensor.transpose(vt_ps[:, u, :], pairs[:, u::2], ident[:])
            evacuate(j < 2, vt_words.rearrange("p (m u) -> p m u", u=2), vt_ps[:].rearrange("p u m -> p m u"))
            return vt_words

        def quantise_values(j, vt_words):
            return quantise(vt_words.bitcast(BF16), P, "vt%d" % j)

        words0 = turn(0, new_tile([P, 2 * P], F32, "vt_words0")[:])
        w_mx = quantise(w_bf[:].rearrange("p q t -> p (q t)"), Q, "w")
        words1 = turn(1, new_tile([P, 2 * P], F32, "vt_words1")[:])
        vt_mx = [quantise_values(0, words0), quantise_values(1, words1)]

        me_second = [memory_product(1, j) for j in range(PACK)]
        for j in range(2):
            evacuate(True, mem[:, j * M + BANK : (j + 1) * M], me_second[j][:])
        gather(False, got_vals[2][:], val_pool[2][:], idx[:])
        gather(False, got_vals[3][:], val_pool[3][:], idx[:])
        for j in range(2, PACK):
            evacuate(True, mem[:, j * M + BANK : (j + 1) * M], me_second[j][:])
        late = new_tile([P, PACK, Q], F32, "late", reuse="val_pool3")
        vt_mx.append(quantise_values(2, turn(2, late[:, 0, :])))
        vt_mx.append(quantise_values(3, turn(3, new_tile([P, 2 * P], F32, "vt_words3")[:])))

        y = new_tile([P, PACK, Q], F32, "y")
        out_rows = out_0.rearrange("(p j) q -> p j q", j=PACK)
        w_operand = moving(w_mx)
        o_first = bank([P, 2, Q], 4, "o_first")
        for j in range(2):
            product(o_first[:, j, :], vt_mx[j], slice(0, P), w_operand)
        for j in range(PACK):
            recalled = new_tile([P, Q], F32, "recalled0")[:] if j == 0 else late[:, j, :]
            gather(j == 0, recalled, mem[:, j * M : (j + 1) * M], idx4[:])
            if j < 2:
                o_ps = o_first[:, j, :]
            else:
                o_ps = bank([P, Q], 4 + j, "o_ps%d" % j)[:]
                product(o_ps, vt_mx[j], slice(0, P), w_operand)
            nc.vector.tensor_tensor(out=y[:, j, :], in0=o_ps, in1=recalled, op=MAX)
            if j % 2 == 1:
                nc.sync.dma_start(out_rows[:, j - 1 : j + 1, :], y[:, j - 1 : j + 1, :])

        y_bf = new_tile([P, Q, PACK], BF16, "y_bf")
        interleave(nc.scalar.copy, y_bf[:, :Y_SCALAR, :], y[:, :, :Y_SCALAR])
        interleave(nc.vector.tensor_copy, y_bf[:, Y_SCALAR:, :], y[:, :, Y_SCALAR:])
        y_codes, y_scales = quantise(y_bf[:].rearrange("p q j -> p (q j)"), Q, "y")
        nc.sync.dma_start(out_1[0].rearrange("p c r -> p (c r)").bitcast(I32), y_codes[:].bitcast(I32))
        for quad in range(P // QUAD):
            queue = nc.scalar if quad % 2 == 0 else nc.sync
            queue.dma_start(
                out_2[0, PACK * quad : PACK * (quad + 1), :].bitcast(I32),
                y_scales[QUAD * quad : QUAD * quad + PACK, :].bitcast(I32),
            )
